import numpy as np
import ml_dtypes


def mxq(x, axis, fmt="e4m3"):
    dtype, down = {"e4m3": (ml_dtypes.float8_e4m3fn, 7), "e5m2": (ml_dtypes.float8_e5m2, 14)}[fmt]
    v = np.moveaxis(np.asarray(x, np.float32).astype(ml_dtypes.bfloat16).astype(np.float64), axis, -1)
    blocks = v.reshape(v.shape[:-1] + (-1, 32))
    amax = np.abs(blocks).max(-1, keepdims=True)
    byte = np.maximum(np.where(amax > 0, np.frexp(amax)[1] - 1 + 127, 0) - down, 1)
    scale = np.exp2(byte - 127.0)
    codes = (blocks / scale).astype(np.float32).astype(dtype).astype(np.float64)
    return np.moveaxis((codes * scale).reshape(v.shape), -1, axis)


WIDE = False


def mx_kscale(k):
    if not WIDE:
        return np.ones(k)
    levels = np.array([18, -18])
    if k % 512:
        return np.exp2(np.random.permutation(np.resize(levels, k // 32))).repeat(32)
    a = np.empty((k // 512, 16))
    for p in range(k // 512):
        a[p, :8] = np.random.permutation(np.resize(levels, 8))
        for g in range(8):
            far = levels[np.abs(levels - a[p, g]) >= 10]
            a[p, g + 8] = far[np.random.randint(len(far))]
    return np.exp2(a.ravel()).repeat(32)


def f64(x):
    return np.asarray(x).astype(np.float64)


def striped(idx):
    return np.tile(np.asarray(idx).reshape(-1, 16).T, (8, 1)).astype(np.uint16)


def unstriped(offs):
    return offs[:16].T.reshape(-1).astype(np.int64)


B, N, T, D, R = 2, 512, 2048, 512, 512


def setup_inputs():
    n = np.random.standard_normal
    idx = np.random.permutation(T)[:B * N]
    s = mx_kscale(D)[:, None]
    z = mx_kscale(R)[:, None]
    u = np.ones(T)
    u[idx] = mx_kscale(B * N)
    r = np.random.uniform(0.5, 2.0, T) * u
    x = n((B, D, R))
    teach = np.exp(n((B, R, N)))
    teach = teach / teach.sum(-1, keepdims=True)
    return {
        "xT": (x * s).astype(np.float32),
        "wT": (n((D, T)) * (0.50 / np.sqrt(D)) / s / r).astype(np.float32),
        "y": teach.astype(np.float32),
        "wt": (np.random.uniform(0.5, 1.5, (B, R, 1)) * N / np.sqrt(R) * z).astype(np.float32),
        "ts": np.tile(r, (128, 1)).astype(np.float32),
        "kb": np.tile(0.5 * n(T), (128, 1)).astype(np.float32),
        "xm": (x.transpose(0, 2, 1) / z).astype(np.float32),
        "offs": striped(idx),
    }


def reference(xT, wT, y, wt, ts, kb, xm, offs):
    idx = unstriped(offs)
    pick = lambda x: x[:, idx].reshape(x.shape[0], B, N).transpose(1, 0, 2)
    w = pick(f64(wT))
    a = mxq(f64(xT), 1, "e4m3").transpose(0, 2, 1) @ mxq(w, 1, "e4m3")
    ts_ = pick(f64(ts))[:, :1, :]
    a = a * ts_
    a = a + pick(f64(kb))[:, :1, :]
    e = np.exp(a - a.max(-1, keepdims=True))
    g = f64(wt) * (e / e.sum(-1, keepdims=True) - f64(y))
    g = g * ts_
    dw = mxq(f64(xm), 1, "e4m3").transpose(0, 2, 1) @ mxq(g, 1, "e5m2")
    gw = np.zeros((D, T))
    gw[:, idx] = dw.transpose(1, 0, 2).reshape(D, B * N)
    gx = mxq(g, 2, "e5m2") @ mxq(w, 2, "e4m3").transpose(0, 2, 1)
    return gw, gx

@@ -1,0 +1,313 @@
+from contextlib import ExitStack
+
+import concourse.mybir as mybir
+from concourse.masks import make_identity
+
+B, N, T, D, R = 2, 512, 2048, 512, 512
+P = 128
+FLOPS = 3 * 2 * B * D * R * N
+BYTES = 4 * (3 * B * D * R + D * T + B * R + 2 * T + D * T + B * R * D) + 2 * P * B * N // 16
+
+F32 = mybir.dt.float32
+BF16 = mybir.dt.bfloat16
+U32 = mybir.dt.uint32
+U16 = mybir.dt.uint16
+U8 = mybir.dt.uint8
+E4M3 = mybir.dt.float8_e4m3fn_x4
+E5M2 = mybir.dt.float8_e5m2_x4
+ALU = mybir.AluOpType
+ACT = mybir.ActivationFunctionType
+AXIS = mybir.AxisListType
+
+CHUNK = 512
+W_CAST = ["s", "s", "s", "s", "s", "s", "sv", "sv"]
+
+
+def tile_attend_gkl_wx_ts_kb_kernel(tc, xT, wT, y, wt, ts, kb, xm, offs, out_0, out_1):
+    nc = tc.nc
+    with ExitStack() as ctx:
+        keep = ctx.enter_context(tc.tile_pool(name="keep", bufs=1))
+        arena = ctx.enter_context(tc.tile_pool(name="arena", bufs=1))
+        psum = ctx.enter_context(tc.psum_pool(name="psum", bufs=1))
+
+        def at(name, kib, cols, dtype):
+            return arena.tile([P, cols], dtype, name=name, offset=int(kib * 1024), align_bytes=64)
+
+        def bank(name, n):
+            return psum.tile([P, 512], F32, name=name, offset=n * 2048)
+
+        def copy(engine, out, in_):
+            if engine == "s":
+                nc.scalar.copy(out, in_)
+            elif engine == "v":
+                nc.vector.tensor_copy(out, in_)
+            else:
+                nc.gpsimd.tensor_scalar(out, in_, 1.0, 0.0, ALU.mult, ALU.add)
+
+        def quantize(name, src, fmt, pieces):
+            codes = keep.tile([P, 512], U32, name=name + "_codes", align_bytes=64)
+            scales = keep.tile([P, 512], U8, name=name + "_scales", align_bytes=64)
+            step = 512 // pieces
+            for c in range(0, 512, step):
+                nc.vector.quantize_mx(codes[:, c:c + step].bitcast(fmt), scales[:, c:c + step], src[:, 4 * c:4 * (c + step)])
+            return codes, scales, fmt
+
+        def matmul(out, lhs, lhs_cols, rhs, rhs_cols):
+            nc.tensor.matmul_mx(
+                out,
+                lhsT=lhs[0][:, lhs_cols].bitcast(lhs[2]), lhsT_scale=lhs[1][:, lhs_cols],
+                rhs=rhs[0][:, rhs_cols].bitcast(rhs[2]), rhs_scale=rhs[1][:, rhs_cols],
+                start=True, stop=True,
+            )
+
+        def interleave(dst, raw, engine, pieces):
+            src_v = raw[:].rearrange("p (j c) -> p c j", j=4)
+            dst_v = dst[:].rearrange("p (c j) -> p c j", j=4)
+            step = 512 // pieces
+            for c in range(0, 512, step):
+                copy(engine, dst_v[:, c:c + step, :], src_v[:, c:c + step, :])
+            return dst
+
+        offsets = keep.tile([P, B * N // 16], U16, name="offsets")
+        nc.sync.dma_start(offsets[:], offs)
+
+        def listed(window, b):
+            return window.indirect(offsets[:, b * (N // 16):(b + 1) * (N // 16)])
+
+        ts_win, kb_win = at("ts_win", 32, T, F32), at("kb_win", 40, T, F32)
+        wt_rows = keep.tile([P, P], F32, name="wt_rows")
+        nc.vector.memset(wt_rows[:], 0.0)
+        nc.vector.memset(ts_win[:], 0.0)
+        nc.vector.memset(kb_win[:], 0.0)
+        warm = keep.tile([P, 1], F32, name="warm")
+        nc.scalar.activation(warm[:], wt_rows[:, 0:1], ACT.Exp)
+        nc.scalar.dma_start(ts_win[0:1, :], ts[0:1, :])
+        nc.scalar.dma_start(kb_win[1:2, :], kb[1:2, :])
+        nc.scalar.dma_start(wt_rows[0:4 * B, :], wt.rearrange("b (j p) o -> (b j) (p o)", p=P))
+        ident = keep.tile([P, P], F32, name="ident")
+        make_identity(nc, ident[:])
+
+        w_rows = wT.rearrange("(p u e) c -> p u e c", u=2, e=2)
+        w_raw = []
+        for u in range(2):
+            for c in range(0, T, CHUNK):
+                raw = at("w_raw%d" % len(w_raw), 4 * len(w_raw), 2 * CHUNK, F32)
+                nc.sync.dma_start(raw[:].rearrange("p (e c) -> p e c", e=2), w_rows[:, u, :, c:c + CHUNK])
+                w_raw.append(raw)
+        x_raw, y_raw, xm_raw = [], [], []
+        for b in range(B):
+            x_raw.append(at("x_raw%d" % b, 76 + 8 * b, 2048, F32))
+            y_raw.append(at("y_raw%d" % b, 92 + 8 * b, 2048, F32))
+            xm_raw.append(at("xm_raw%d" % b, 108 + 8 * b, 2048, F32))
+
+        def load_x(b):
+            nc.sync.dma_start(x_raw[b][:], xT[b].rearrange("(p j) r -> p (j r)", j=4))
+
+        def load_y(b):
+            nc.sync.dma_start(y_raw[b][:].rearrange("p (j i) -> p j i", j=4), y[b].rearrange("(j p) i -> p j i", p=P))
+
+        def load_xm(b):
+            nc.sync.dma_start(xm_raw[b][:], xm[b].rearrange("(p j) d -> p (j d)", j=4))
+
+        load_x(0)
+        load_y(0)
+        load_x(1)
+        load_xm(0)
+        load_y(1)
+        load_xm(1)
+
+        w_pairs = [at("w_pairs%d" % u, 60 + 8 * u, 2 * T, BF16) for u in range(2)]
+        for n, raw in enumerate(w_raw):
+            u, c = n // (T // CHUNK), (n % (T // CHUNK)) * CHUNK
+            engines = W_CAST[n]
+            step = CHUNK // len(engines)
+            for k, engine in enumerate(engines):
+                copy(engine,
+                     w_pairs[u][:].rearrange("p (c e) -> p c e", e=2)[:, c + k * step:c + (k + 1) * step, :],
+                     raw[:].rearrange("p (e c) -> p c e", e=2)[:, k * step:(k + 1) * step, :])
+
+        wt_bank = bank("wt_bank", 7)
+        nc.tensor.transpose(wt_bank[:, 0:P], wt_rows[:], ident[:])
+        wt_cols = keep.tile([P, 4 * B], F32, name="wt_cols")
+        nc.scalar.copy(wt_cols[:], wt_bank[:, 0:4 * B])
+
+        windows = [keep.tile([P, T], F32, name="window%d" % k) for k in range(4)]
+        for window in windows:
+            for c in range(0, T, 512):
+                nc.gpsimd.memset(window[:, c:c + 512], 0.0)
+        minus_one = keep.tile([P, 1], F32, name="minus_one")
+        nc.gpsimd.memset(minus_one[:], -1.0)
+
+        def gather(b, picked, u):
+            nc.vector.tensor_copy(
+                picked[:, u * N:(u + 1) * N].rearrange("p (t g a) -> p g t a", t=4, a=8),
+                listed(w_pairs[u][:].bitcast(U32), b))
+
+        def token_columns(b):
+            ts_g, kb_g, both = [at("tok%d_%d" % (b, i), 48 + 6 * b + 2 * i, N, F32) for i in range(3)]
+            nc.vector.tensor_copy(ts_g[:], listed(ts_win[:], b))
+            nc.vector.tensor_copy(kb_g[:], listed(kb_win[:], b))
+            nc.vector.tensor_tensor(
+                both[:].rearrange("p (t g a) -> p t g a", t=4, a=8),
+                ts_g[:].rearrange("p (g t a) -> p t g a", t=4, a=8),
+                kb_g[:].rearrange("p (g t a) -> p t g a", t=4, a=8), ALU.add)
+            turned = bank("tok_bank%d" % b, 5 + b)
+            for t in range(4):
+                nc.tensor.transpose(turned[:, t * P:(t + 1) * P], both[:, t * P:(t + 1) * P], ident[:])
+            cols = keep.tile([P, 4, 2], F32, name="tok_cols%d" % b)
+            nc.vector.tensor_copy(cols[:], turned[:].rearrange("p (t q) -> p t q", t=4)[:, :, 0:2])
+            return cols
+
+        def quantize_w(b, picked, w_in):
+            copy("v", w_in[:].rearrange("p (s u e) -> p s u e", u=2, e=2),
+                 picked[:].bitcast(BF16).rearrange("p (u s e) -> p s u e", u=2, e=2))
+            return quantize("w%d" % b, w_in, E4M3, 2)
+
+        def scores(b, half, w_q, x_q, cols):
+            a_t = at("a_t%d_%d" % (b, half), 8 * b + 4 * half, 1024, F32)
+            for tp in range(2):
+                acc = bank("scores%d_%d_%d" % (b, half, tp), 4 * b + 2 * half + tp)
+                for q in range(2):
+                    t = 2 * tp + q
+                    matmul(acc[:, q * 256:(q + 1) * 256], w_q, slice(t * P, (t + 1) * P), x_q, slice(half * 256, (half + 1) * 256))
+                for q in range(2):
+                    t = 2 * tp + q
+                    nc.scalar.activation(a_t[:, t * 256:(t + 1) * 256], acc[:, q * 256:(q + 1) * 256], ACT.Identity,
+                                         bias=cols[:, t, 1:2], scale=cols[:, t, 0:1])
+            return a_t
+
+        def targets(b, j):
+            target = at("target%d_%d" % (b, j), 16 + 8 * b + 2 * j, N, F32)
+            nc.gpsimd.tensor_scalar(
+                target[:].rearrange("p (t g a) -> p t g a", t=4, a=8),
+                y_raw[b][:, j * N:(j + 1) * N].rearrange("p (g t a) -> p t g a", t=4, a=8),
+                wt_cols[:, 4 * b + j:4 * b + j + 1], -1.0, ALU.mult, ALU.mult)
+            return target
+
+        def row_max(b, j, a_t):
+            rows = bank("rows%d_%d" % (b, j), 4 * b + j)
+            jj = j % 2
+            for t in range(4):
+                nc.tensor.transpose(rows[:, t * P:(t + 1) * P], a_t[:, t * 256 + jj * P:t * 256 + (jj + 1) * P], ident[:])
+            neg_max = keep.tile([P, 1], F32, name="neg_max%d_%d" % (b, j))
+            nc.vector.tensor_reduce(neg_max[:], rows[:], AXIS.X, ALU.max, negate=True)
+            return rows, neg_max
+
+        def weighted(b, j, rows, neg_max):
+            total = keep.tile([P, 1], F32, name="total%d_%d" % (b, j))
+            inverse = keep.tile([P, 1], F32, name="inverse%d_%d" % (b, j))
+            prob = at("prob%d_%d" % (b, j), 32 + 8 * b + 2 * j, N, F32)
+            nc.scalar.activation(prob[:], rows[:], ACT.Exp, bias=neg_max[:], scale=1.0, accum_out=total[:])
+            if b == 0:
+                nc.vector.reciprocal(inverse[:], total[:])
+            else:
+                nc.gpsimd.tensor_tensor(inverse[:], total[:], minus_one[:], ALU.pow)
+            nc.gpsimd.tensor_scalar(prob[:], prob[:], inverse[:], wt_cols[:, 4 * b + j:4 * b + j + 1], ALU.mult, ALU.mult)
+            return prob
+
+        def turn_and_scale(b, half, target, prob, cols, h_t):
+            h_tv = h_t[:].rearrange("p (t u m e) -> p t u m e", t=4, u=2, e=2)
+            for tp in range(2):
+                turned = bank("turned%d_%d_%d" % (b, half, tp), 4 * b + 2 * half + tp)
+                for term, tiles in enumerate((target, prob)):
+                    for jj in range(2):
+                        for q in range(2):
+                            t = 2 * tp + q
+                            nc.tensor.matmul(
+                                turned[:, q * 256 + jj * P:q * 256 + (jj + 1) * P], tiles[2 * half + jj][:, t * P:(t + 1) * P], ident[:],
+                                start=(term, jj, q) == (0, 0, 0), stop=(term, jj, q) == (1, 1, 1), is_transpose=True)
+                for q in range(2):
+                    t = 2 * tp + q
+                    nc.scalar.activation(
+                        h_tv[:, t, :, half * 64:(half + 1) * 64, :],
+                        turned[:, q * 256:(q + 1) * 256].rearrange("p (m u e) -> p u m e", u=2, e=2),
+                        ACT.Copy, scale=cols[:, t, 0:1])
+
+        def quantize_h(b, h_t):
+            h_in = at("h_in%d" % b, 76 + 8 * b, 2048, BF16)
+            h_words = h_t[:].bitcast(F32)
+            h_inv = h_in[:].bitcast(F32).rearrange("p (g t a u) -> p t g a u", t=4, a=8, u=2)
+            for tp in range(2):
+                turned = bank("h_words%d_%d" % (b, tp), 4 * b + tp)
+                for q in range(4):
+                    nc.tensor.transpose(turned[:, q * P:(q + 1) * P], h_words[:, (4 * tp + q) * P:(4 * tp + q + 1) * P], ident[:])
+                for q in range(2):
+                    nc.scalar.copy(h_inv[:, 2 * tp + q], turned[:, q * 256:(q + 1) * 256].rearrange("p (u g a) -> p g a u", u=2, a=8))
+            return quantize("h%d" % b, h_in, E5M2, 1)
+
+        def quantize_xm(b):
+            return quantize("xm%d" % b, interleave(at("xm_in%d" % b, 124 + 4 * b, 2048, BF16), xm_raw[b], "g", 4), E4M3, 1)
+
+        def table_gradient(b, k, n, xm_q, h_q):
+            acc = bank("dw%d_%d" % (b, k), n)
+            matmul(acc[:], xm_q, slice(k * P, (k + 1) * P), h_q, slice(0, N))
+            staged = at("dw_staged%d_%d" % (b, k), 48 + 2 * ((4 * b + k) % 6), N, F32)
+            nc.scalar.copy(staged[:], acc[:])
+            nc.vector.tensor_copy(listed(windows[k][:], b), staged[:])
+            if b == B - 1:
+                nc.sync.dma_start(out_0[k * P:(k + 1) * P, :], windows[k][:])
+
+        def quantize_back(b, picked, h_t, banks):
+            w_t = at("w_t%d" % b, 92 + 4 * b, 2048, BF16)
+            w_tv = w_t[:].rearrange("p (m u e t) -> p u m e t", u=2, e=2, t=4)
+            words = picked[:].bitcast(F32)
+            for u in range(2):
+                turned = bank("w_words%d_%d" % (b, u), banks[u])
+                for t in range(4):
+                    nc.tensor.transpose(turned[:, t * P:(t + 1) * P], words[:, (4 * u + t) * P:(4 * u + t + 1) * P], ident[:])
+                nc.scalar.copy(w_tv[:, u], turned[:].bitcast(BF16).rearrange("p (t m e) -> p m e t", t=4, e=2))
+            h_ti = at("h_ti%d" % b, 80 + 8 * b, 2048, BF16)
+            for u in range(2):
+                for c in range(0, P, 64):
+                    copy("g", h_ti[:].rearrange("p (m u e t) -> p u m e t", u=2, e=2, t=4)[:, u, c:c + 64],
+                         h_t[:].rearrange("p (t u m e) -> p u m e t", t=4, u=2, e=2)[:, u, c:c + 64])
+            return quantize("h_t%d" % b, h_ti, E5M2, 1), quantize("w_t%d" % b, w_t, E4M3, 1)
+
+        def row_gradient(b, j, n, h_tq, w_tq):
+            acc = bank("gx%d_%d" % (b, j), n)
+            matmul(acc[:], h_tq, slice(j * P, (j + 1) * P), w_tq, slice(0, D))
+            staged = at("gx_staged%d_%d" % (b, j), 60 + 8 * b + 2 * j, D, F32)
+            nc.scalar.copy(staged[:], acc[:])
+            nc.scalar.dma_start(out_1[b, j * P:(j + 1) * P, :], staged[:])
+
+        picked0 = at("picked0", 132, 2 * N, U32)
+        gather(0, picked0, 0)
+        gather(0, picked0, 1)
+        w_q0 = quantize_w(0, picked0, at("w_in0", 136, 2048, BF16))
+        x_q0 = quantize("x0", interleave(at("x_in0", 140, 2048, BF16), x_raw[0], "s", 2), E4M3, 2)
+        cols = [token_columns(b) for b in range(B)]
+        h_t = [at("h_t%d" % b, 144 + 4 * b, 2048, BF16) for b in range(B)]
+
+        a_t0 = [scores(0, half, w_q0, x_q0, cols[0]) for half in range(2)]
+        target0 = [targets(0, j) for j in range(4)]
+        prob0 = [weighted(0, j, *row_max(0, j, a_t0[j // 2])) for j in range(4)]
+        turn_and_scale(0, 0, target0, prob0, cols[0], h_t[0])
+        turn_and_scale(0, 1, target0, prob0, cols[0], h_t[0])
+        xm_q0 = quantize_xm(0)
+        h_q0 = quantize_h(0, h_t[0])
+        table_gradient(0, 0, 2, xm_q0, h_q0)
+        picked1 = at("picked1", 140, 2 * N, U32)
+        gather(1, picked1, 0)
+        gather(1, picked1, 1)
+        w_q1 = quantize_w(1, picked1, at("w_in1", 136, 2048, BF16))
+        x_q1 = quantize("x1", interleave(at("x_in1", 152, 2048, BF16), x_raw[1], "v", 2), E4M3, 2)
+        a_t1 = [scores(1, half, w_q1, x_q1, cols[1]) for half in range(2)]
+        maxes1 = [row_max(1, j, a_t1[j // 2]) for j in range(4)]
+        target1 = [targets(1, j) for j in range(4)]
+        prob1 = [weighted(1, j, *maxes1[j]) for j in range(4)]
+        table_gradient(0, 1, 6, xm_q0, h_q0)
+        table_gradient(0, 2, 7, xm_q0, h_q0)
+        turn_and_scale(1, 0, target1, prob1, cols[1], h_t[1])
+        turn_and_scale(1, 1, target1, prob1, cols[1], h_t[1])
+        xm_q1 = quantize_xm(1)
+        h_q1 = quantize_h(1, h_t[1])
+        table_gradient(0, 3, 4, xm_q0, h_q0)
+        table_gradient(1, 0, 5, xm_q1, h_q1)
+        back0 = quantize_back(0, picked0, h_t[0], (0, 1))
+        table_gradient(1, 1, 6, xm_q1, h_q1)
+        back1 = quantize_back(1, picked1, h_t[1], (4, 5))
+        table_gradient(1, 2, 7, xm_q1, h_q1)
+        table_gradient(1, 3, 2, xm_q1, h_q1)
+        for b, back in enumerate((back0, back1)):
+            for j in range(4):
+                row_gradient(b, j, (3, 0, 1, 6)[j], *back)

@@ -20,7 +20,9 @@ ACT = mybir.ActivationFunctionType
 AXIS = mybir.AxisListType
 
 CHUNK = 512
-W_CAST = ["s", "s", "s", "s", "s", "s", "sv", "sv"]
+OFF = dict(y1=24, m0=124, m1=128, w0=8, w1=40, h0=76, h1=84)
+LOADS = [(0, 0), (1, 0), (0, 1), (1, 1), (2, 0), (2, 1)]
+W_CAST = ["s","s","s","s","s","s","s","sv"]
 
 
 def tile_attend_gkl_wx_ts_kb_kernel(tc, xT, wT, y, wt, ts, kb, xm, offs, out_0, out_1):
@@ -39,10 +41,8 @@ def tile_attend_gkl_wx_ts_kb_kernel(tc, xT, wT, y, wt, ts, kb, xm, offs, out_0, 
         def copy(engine, out, in_):
             if engine == "s":
                 nc.scalar.copy(out, in_)
-            elif engine == "v":
-                nc.vector.tensor_copy(out, in_)
             else:
-                nc.gpsimd.tensor_scalar(out, in_, 1.0, 0.0, ALU.mult, ALU.add)
+                nc.vector.tensor_copy(out, in_)
 
         def quantize(name, src, fmt, pieces):
             codes = keep.tile([P, 512], U32, name=name + "_codes", align_bytes=64)
@@ -60,12 +60,12 @@ def tile_attend_gkl_wx_ts_kb_kernel(tc, xT, wT, y, wt, ts, kb, xm, offs, out_0, 
                 start=True, stop=True,
             )
 
-        def interleave(dst, raw, engine, pieces):
-            src_v = raw[:].rearrange("p (j c) -> p c j", j=4)
-            dst_v = dst[:].rearrange("p (c j) -> p c j", j=4)
-            step = 512 // pieces
-            for c in range(0, 512, step):
-                copy(engine, dst_v[:, c:c + step, :], src_v[:, c:c + step, :])
+        def interleave(dst, raw, engines):
+            src_v = raw[:].rearrange("p (j c i) -> p c j i", j=4, i=4)
+            dst_v = dst[:].rearrange("p (c i j) -> p c j i", j=4, i=4)
+            step = 128 // len(engines)
+            for k, engine in enumerate(engines):
+                copy(engine, dst_v[:, k * step:(k + 1) * step], src_v[:, k * step:(k + 1) * step])
             return dst
 
         offsets = keep.tile([P, B * N // 16], U16, name="offsets")
@@ -109,34 +109,31 @@ def tile_attend_gkl_wx_ts_kb_kernel(tc, xT, wT, y, wt, ts, kb, xm, offs, out_0, 
         def load_xm(b):
             nc.sync.dma_start(xm_raw[b][:], xm[b].rearrange("(p j) d -> p (j d)", j=4))
 
-        load_x(0)
-        load_y(0)
-        load_x(1)
-        load_xm(0)
-        load_y(1)
-        load_xm(1)
+        for load, b in LOADS:
+            (load_x, load_y, load_xm)[load](b)
 
         w_pairs = [at("w_pairs%d" % u, 60 + 8 * u, 2 * T, BF16) for u in range(2)]
         for n, raw in enumerate(w_raw):
             u, c = n // (T // CHUNK), (n % (T // CHUNK)) * CHUNK
             engines = W_CAST[n]
-            step = CHUNK // len(engines)
+            step = CHUNK // 4 // len(engines)
             for k, engine in enumerate(engines):
                 copy(engine,
-                     w_pairs[u][:].rearrange("p (c e) -> p c e", e=2)[:, c + k * step:c + (k + 1) * step, :],
-                     raw[:].rearrange("p (e c) -> p c e", e=2)[:, k * step:(k + 1) * step, :])
+                     w_pairs[u][:].rearrange("p (c i e) -> p c e i", e=2, i=4)[:, c // 4 + k * step:c // 4 + (k + 1) * step],
+                     raw[:].rearrange("p (e c i) -> p c e i", e=2, i=4)[:, k * step:(k + 1) * step])
 
         wt_bank = bank("wt_bank", 7)
         nc.tensor.transpose(wt_bank[:, 0:P], wt_rows[:], ident[:])
         wt_cols = keep.tile([P, 4 * B], F32, name="wt_cols")
-        nc.scalar.copy(wt_cols[:], wt_bank[:, 0:4 * B])
+        nc.vector.tensor_copy(wt_cols[:], wt_bank[:, 0:4 * B])
+
+        neg_wt_cols = keep.tile([P, 4 * B], F32, name="neg_wt_cols")
+        nc.vector.tensor_scalar_mul(neg_wt_cols[:], wt_bank[:, 0:4 * B], -1.0)
 
         windows = [keep.tile([P, T], F32, name="window%d" % k) for k in range(4)]
         for window in windows:
             for c in range(0, T, 512):
                 nc.gpsimd.memset(window[:, c:c + 512], 0.0)
-        minus_one = keep.tile([P, 1], F32, name="minus_one")
-        nc.gpsimd.memset(minus_one[:], -1.0)
 
         def gather(b, picked, u):
             nc.vector.tensor_copy(
@@ -158,12 +155,12 @@ def tile_attend_gkl_wx_ts_kb_kernel(tc, xT, wT, y, wt, ts, kb, xm, offs, out_0, 
             nc.vector.tensor_copy(cols[:], turned[:].rearrange("p (t q) -> p t q", t=4)[:, :, 0:2])
             return cols
 
-        def quantize_w(b, picked, w_in):
-            copy("v", w_in[:].rearrange("p (s u e) -> p s u e", u=2, e=2),
+        def quantize_w(b, picked, w_in, engine):
+            copy(engine, w_in[:].rearrange("p (s u e) -> p s u e", u=2, e=2),
                  picked[:].bitcast(BF16).rearrange("p (u s e) -> p s u e", u=2, e=2))
             return quantize("w%d" % b, w_in, E4M3, 2)
 
-        def scores(b, half, w_q, x_q, cols):
+        def scores(b, half, w_q, x_q, cols, engines):
             a_t = at("a_t%d_%d" % (b, half), 8 * b + 4 * half, 1024, F32)
             for tp in range(2):
                 acc = bank("scores%d_%d_%d" % (b, half, tp), 4 * b + 2 * half + tp)
@@ -172,16 +169,21 @@ def tile_attend_gkl_wx_ts_kb_kernel(tc, xT, wT, y, wt, ts, kb, xm, offs, out_0, 
                     matmul(acc[:, q * 256:(q + 1) * 256], w_q, slice(t * P, (t + 1) * P), x_q, slice(half * 256, (half + 1) * 256))
                 for q in range(2):
                     t = 2 * tp + q
-                    nc.scalar.activation(a_t[:, t * 256:(t + 1) * 256], acc[:, q * 256:(q + 1) * 256], ACT.Identity,
-                                         bias=cols[:, t, 1:2], scale=cols[:, t, 0:1])
+                    dst, src = a_t[:, t * 256:(t + 1) * 256], acc[:, q * 256:(q + 1) * 256]
+                    if engines[tp] == "s":
+                        nc.scalar.activation(dst, src, ACT.Identity, bias=cols[:, t, 1:2], scale=cols[:, t, 0:1])
+                    else:
+                        nc.vector.tensor_scalar(dst, src, cols[:, t, 0:1], cols[:, t, 1:2], ALU.mult, ALU.add)
             return a_t
 
-        def targets(b, j):
-            target = at("target%d_%d" % (b, j), 16 + 8 * b + 2 * j, N, F32)
-            nc.gpsimd.tensor_scalar(
-                target[:].rearrange("p (t g a) -> p t g a", t=4, a=8),
-                y_raw[b][:, j * N:(j + 1) * N].rearrange("p (g t a) -> p t g a", t=4, a=8),
-                wt_cols[:, 4 * b + j:4 * b + j + 1], -1.0, ALU.mult, ALU.mult)
+        def targets(b, j, engine):
+            target = at("target%d_%d" % (b, j), (16, OFF["y1"])[b] + 2 * j, N, F32)
+            dst = target[:].rearrange("p (t g a) -> p t g a", t=4, a=8)
+            src = y_raw[b][:, j * N:(j + 1) * N].rearrange("p (g t a) -> p t g a", t=4, a=8)
+            if engine == "s":
+                nc.scalar.activation(dst, src, ACT.Copy, scale=neg_wt_cols[:, 4 * b + j:4 * b + j + 1])
+            else:
+                nc.vector.tensor_scalar_mul(dst, src, neg_wt_cols[:, 4 * b + j:4 * b + j + 1])
             return target
 
         def row_max(b, j, a_t):
@@ -193,17 +195,30 @@ def tile_attend_gkl_wx_ts_kb_kernel(tc, xT, wT, y, wt, ts, kb, xm, offs, out_0, 
             nc.vector.tensor_reduce(neg_max[:], rows[:], AXIS.X, ALU.max, negate=True)
             return rows, neg_max
 
-        def weighted(b, j, rows, neg_max):
+        def exponentials(b, j, rows, neg_max, total):
+            prob = at("prob%d_%d" % (b, j), 32 + 8 * b + 2 * j, N, F32)
+            nc.scalar.activation(prob[:], rows[:], ACT.Exp, bias=neg_max[:], scale=1.0, accum_out=total)
+            return prob
+
+        def weighted_on_vector(b, j, maxes):
+            rows, neg_max = maxes[j]
             total = keep.tile([P, 1], F32, name="total%d_%d" % (b, j))
             inverse = keep.tile([P, 1], F32, name="inverse%d_%d" % (b, j))
-            prob = at("prob%d_%d" % (b, j), 32 + 8 * b + 2 * j, N, F32)
-            nc.scalar.activation(prob[:], rows[:], ACT.Exp, bias=neg_max[:], scale=1.0, accum_out=total[:])
-            if b == 0:
-                nc.vector.reciprocal(inverse[:], total[:])
-            else:
-                nc.gpsimd.tensor_tensor(inverse[:], total[:], minus_one[:], ALU.pow)
-            nc.gpsimd.tensor_scalar(prob[:], prob[:], inverse[:], wt_cols[:, 4 * b + j:4 * b + j + 1], ALU.mult, ALU.mult)
+            prob = exponentials(b, j, rows, neg_max, total[:])
+            nc.vector.reciprocal(inverse[:], total[:])
+            nc.vector.tensor_scalar(prob[:], prob[:], inverse[:], wt_cols[:, 4 * b + j:4 * b + j + 1], ALU.mult, ALU.mult)
             return prob
+
+        def weighted_on_scalar(b, js, maxes):
+            total = keep.tile([P, len(js)], F32, name="totals%d_%d" % (b, js[0]))
+            inverse = keep.tile([P, len(js)], F32, name="inverses%d_%d" % (b, js[0]))
+            factor = keep.tile([P, len(js)], F32, name="factors%d_%d" % (b, js[0]))
+            probs = [exponentials(b, j, *maxes[j], total[:, n:n + 1]) for n, j in enumerate(js)]
+            nc.vector.reciprocal(inverse[:], total[:])
+            nc.vector.tensor_tensor(factor[:], inverse[:], wt_cols[:, 4 * b + js[0]:4 * b + js[-1] + 1], ALU.mult)
+            for n, prob in enumerate(probs):
+                nc.scalar.activation(prob[:], prob[:], ACT.Copy, scale=factor[:, n:n + 1])
+            return probs
 
         def turn_and_scale(b, half, target, prob, cols, h_t):
             h_tv = h_t[:].rearrange("p (t u m e) -> p t u m e", t=4, u=2, e=2)
@@ -235,20 +250,23 @@ def tile_attend_gkl_wx_ts_kb_kernel(tc, xT, wT, y, wt, ts, kb, xm, offs, out_0, 
                     nc.scalar.copy(h_inv[:, 2 * tp + q], turned[:, q * 256:(q + 1) * 256].rearrange("p (u g a) -> p g a u", u=2, a=8))
             return quantize("h%d" % b, h_in, E5M2, 1)
 
-        def quantize_xm(b):
-            return quantize("xm%d" % b, interleave(at("xm_in%d" % b, 124 + 4 * b, 2048, BF16), xm_raw[b], "g", 4), E4M3, 1)
+        def quantize_xm(b, engine):
+            return quantize("xm%d" % b, interleave(at("xm_in%d" % b, OFF["m%d" % b], 2048, BF16), xm_raw[b], engine), E4M3, 1)
 
-        def table_gradient(b, k, n, xm_q, h_q):
+        def table_gradient(b, k, n, xm_q, h_q, pieces):
             acc = bank("dw%d_%d" % (b, k), n)
             matmul(acc[:], xm_q, slice(k * P, (k + 1) * P), h_q, slice(0, N))
             staged = at("dw_staged%d_%d" % (b, k), 48 + 2 * ((4 * b + k) % 6), N, F32)
             nc.scalar.copy(staged[:], acc[:])
-            nc.vector.tensor_copy(listed(windows[k][:], b), staged[:])
+            step = N // pieces
+            for c in range(0, N, step):
+                part = offsets[:, (b * N + c) // 16:(b * N + c + step) // 16]
+                nc.vector.tensor_copy(windows[k][:].indirect(part), staged[:, c:c + step])
             if b == B - 1:
                 nc.sync.dma_start(out_0[k * P:(k + 1) * P, :], windows[k][:])
 
-        def quantize_back(b, picked, h_t, banks):
-            w_t = at("w_t%d" % b, 92 + 4 * b, 2048, BF16)
+        def quantize_w_turned(b, picked, banks):
+            w_t = at("w_t%d" % b, OFF["w%d" % b], 2048, BF16)
             w_tv = w_t[:].rearrange("p (m u e t) -> p u m e t", u=2, e=2, t=4)
             words = picked[:].bitcast(F32)
             for u in range(2):
@@ -256,12 +274,14 @@ def tile_attend_gkl_wx_ts_kb_kernel(tc, xT, wT, y, wt, ts, kb, xm, offs, out_0, 
                 for t in range(4):
                     nc.tensor.transpose(turned[:, t * P:(t + 1) * P], words[:, (4 * u + t) * P:(4 * u + t + 1) * P], ident[:])
                 nc.scalar.copy(w_tv[:, u], turned[:].bitcast(BF16).rearrange("p (t m e) -> p m e t", t=4, e=2))
-            h_ti = at("h_ti%d" % b, 80 + 8 * b, 2048, BF16)
+            return quantize("w_t%d" % b, w_t, E4M3, 1)
+
+        def quantize_h_turned(b, h_t, engines):
+            h_ti = at("h_ti%d" % b, OFF["h%d" % b], 2048, BF16)
             for u in range(2):
-                for c in range(0, P, 64):
-                    copy("g", h_ti[:].rearrange("p (m u e t) -> p u m e t", u=2, e=2, t=4)[:, u, c:c + 64],
-                         h_t[:].rearrange("p (t u m e) -> p u m e t", t=4, u=2, e=2)[:, u, c:c + 64])
-            return quantize("h_t%d" % b, h_ti, E5M2, 1), quantize("w_t%d" % b, w_t, E4M3, 1)
+                copy(engines[u], h_ti[:].rearrange("p (m u e t) -> p u m e t", u=2, e=2, t=4)[:, u],
+                     h_t[:].rearrange("p (t u m e) -> p u m e t", t=4, u=2, e=2)[:, u])
+            return quantize("h_t%d" % b, h_ti, E5M2, 1)
 
         def row_gradient(b, j, n, h_tq, w_tq):
             acc = bank("gx%d_%d" % (b, j), n)
@@ -270,44 +290,70 @@ def tile_attend_gkl_wx_ts_kb_kernel(tc, xT, wT, y, wt, ts, kb, xm, offs, out_0, 
             nc.scalar.copy(staged[:], acc[:])
             nc.scalar.dma_start(out_1[b, j * P:(j + 1) * P, :], staged[:])
 
+        h_t = [at("h_t%d" % b, 144 + 4 * b, 2048, BF16) for b in range(B)]
+        a_t, target, maxes, prob = [[{} for b in range(B)] for n in range(4)]
+        cols0 = token_columns(0)
+        x_q0 = quantize("x0", interleave(at("x_in0", 140, 2048, BF16), x_raw[0], "ss"), E4M3, 2)
+        cols1 = token_columns(1)
+        target[0][0] = targets(0, 0, "v")
         picked0 = at("picked0", 132, 2 * N, U32)
         gather(0, picked0, 0)
         gather(0, picked0, 1)
-        w_q0 = quantize_w(0, picked0, at("w_in0", 136, 2048, BF16))
-        x_q0 = quantize("x0", interleave(at("x_in0", 140, 2048, BF16), x_raw[0], "s", 2), E4M3, 2)
-        cols = [token_columns(b) for b in range(B)]
-        h_t = [at("h_t%d" % b, 144 + 4 * b, 2048, BF16) for b in range(B)]
-
-        a_t0 = [scores(0, half, w_q0, x_q0, cols[0]) for half in range(2)]
-        target0 = [targets(0, j) for j in range(4)]
-        prob0 = [weighted(0, j, *row_max(0, j, a_t0[j // 2])) for j in range(4)]
-        turn_and_scale(0, 0, target0, prob0, cols[0], h_t[0])
-        turn_and_scale(0, 1, target0, prob0, cols[0], h_t[0])
-        xm_q0 = quantize_xm(0)
-        h_q0 = quantize_h(0, h_t[0])
-        table_gradient(0, 0, 2, xm_q0, h_q0)
+        w_q0 = quantize_w(0, picked0, at("w_in0", 136, 2048, BF16), "v")
+        target[0][1] = targets(0, 1, "v")
+        a_t[0][1] = scores(0, 1, w_q0, x_q0, cols0, "ss")
+        a_t[0][0] = scores(0, 0, w_q0, x_q0, cols0, "ss")
+        maxes[0][0] = row_max(0, 0, a_t[0][0])
+        maxes[0][1] = row_max(0, 1, a_t[0][0])
+        x_q1 = quantize("x1", interleave(at("x_in1", 152, 2048, BF16), x_raw[1], "sv"), E4M3, 2)
+        target[0][3] = targets(0, 3, "s")
+        prob[0][0], prob[0][1] = weighted_on_scalar(0, (0, 1), maxes[0])
+        target[1][3] = targets(1, 3, "s")
         picked1 = at("picked1", 140, 2 * N, U32)
         gather(1, picked1, 0)
         gather(1, picked1, 1)
-        w_q1 = quantize_w(1, picked1, at("w_in1", 136, 2048, BF16))
-        x_q1 = quantize("x1", interleave(at("x_in1", 152, 2048, BF16), x_raw[1], "v", 2), E4M3, 2)
-        a_t1 = [scores(1, half, w_q1, x_q1, cols[1]) for half in range(2)]
-        maxes1 = [row_max(1, j, a_t1[j // 2]) for j in range(4)]
-        target1 = [targets(1, j) for j in range(4)]
-        prob1 = [weighted(1, j, *maxes1[j]) for j in range(4)]
-        table_gradient(0, 1, 6, xm_q0, h_q0)
-        table_gradient(0, 2, 7, xm_q0, h_q0)
-        turn_and_scale(1, 0, target1, prob1, cols[1], h_t[1])
-        turn_and_scale(1, 1, target1, prob1, cols[1], h_t[1])
-        xm_q1 = quantize_xm(1)
+        w_q1 = quantize_w(1, picked1, at("w_in1", 156, 2048, BF16), "v")
+        maxes[0][2] = row_max(0, 2, a_t[0][1])
+        maxes[0][3] = row_max(0, 3, a_t[0][1])
+        a_t[1][0] = scores(1, 0, w_q1, x_q1, cols1, "vv")
+        prob[0][2] = weighted_on_vector(0, 2, maxes[0])
+        prob[0][3] = weighted_on_vector(0, 3, maxes[0])
+        maxes[1][0] = row_max(1, 0, a_t[1][0])
+        target[1][0] = targets(1, 0, "v")
+        xm_q0 = quantize_xm(0, "vv")
+        a_t[1][1] = scores(1, 1, w_q1, x_q1, cols1, "vv")
+        target[0][2] = targets(0, 2, "s")
+        maxes[1][3] = row_max(1, 3, a_t[1][1])
+        turn_and_scale(0, 0, target[0], prob[0], cols0, h_t[0])
+        maxes[1][2] = row_max(1, 2, a_t[1][1])
+        target[1][2] = targets(1, 2, "s")
+        turn_and_scale(0, 1, target[0], prob[0], cols0, h_t[0])
+        maxes[1][1] = row_max(1, 1, a_t[1][0])
+        h_q0 = quantize_h(0, h_t[0])
+        table_gradient(0, 1, 0, xm_q0, h_q0, 1)
+        prob[1][2], prob[1][3] = weighted_on_scalar(1, (2, 3), maxes[1])
+        h_tq0 = quantize_h_turned(0, h_t[0], "vs")
+        prob[1][0], prob[1][1] = weighted_on_scalar(1, (0, 1), maxes[1])
+        target[1][1] = targets(1, 1, "v")
+        table_gradient(0, 0, 4, xm_q0, h_q0, 1)
+        xm_q1 = quantize_xm(1, "sv")
+        turn_and_scale(1, 1, target[1], prob[1], cols1, h_t[1])
+        table_gradient(0, 2, 3, xm_q0, h_q0, 1)
+        turn_and_scale(1, 0, target[1], prob[1], cols1, h_t[1])
         h_q1 = quantize_h(1, h_t[1])
-        table_gradient(0, 3, 4, xm_q0, h_q0)
-        table_gradient(1, 0, 5, xm_q1, h_q1)
-        back0 = quantize_back(0, picked0, h_t[0], (0, 1))
-        table_gradient(1, 1, 6, xm_q1, h_q1)
-        back1 = quantize_back(1, picked1, h_t[1], (4, 5))
-        table_gradient(1, 2, 7, xm_q1, h_q1)
-        table_gradient(1, 3, 2, xm_q1, h_q1)
-        for b, back in enumerate((back0, back1)):
-            for j in range(4):
-                row_gradient(b, j, (3, 0, 1, 6)[j], *back)
+        table_gradient(0, 3, 4, xm_q0, h_q0, 1)
+        w_tq1 = quantize_w_turned(1, picked1, (5, 0))
+        h_tq1 = quantize_h_turned(1, h_t[1], "ss")
+        row_gradient(1, 0, 0, h_tq1, w_tq1)
+        table_gradient(1, 0, 3, xm_q1, h_q1, 1)
+        w_tq0 = quantize_w_turned(0, picked0, (4, 7))
+        table_gradient(1, 3, 2, xm_q1, h_q1, 1)
+        table_gradient(1, 1, 5, xm_q1, h_q1, 1)
+        row_gradient(1, 3, 1, h_tq1, w_tq1)
+        row_gradient(1, 2, 3, h_tq1, w_tq1)
+        row_gradient(0, 1, 1, h_tq0, w_tq0)
+        row_gradient(1, 1, 4, h_tq1, w_tq1)
+        row_gradient(0, 0, 1, h_tq0, w_tq0)
+        row_gradient(0, 3, 3, h_tq0, w_tq0)
+        row_gradient(0, 2, 4, h_tq0, w_tq0)
+        table_gradient(1, 2, 7, xm_q1, h_q1, 1)

@@ -20,9 +20,14 @@ ACT = mybir.ActivationFunctionType
 AXIS = mybir.AxisListType
 
 CHUNK = 512
-OFF = dict(y1=24, m0=124, m1=128, w0=8, w1=40, h0=76, h1=84)
-LOADS = [(0, 0), (1, 0), (0, 1), (1, 1), (2, 0), (2, 1)]
-W_CAST = ["s","s","s","s","s","s","s","sv"]
+X_LOADS = (2, 1)
+W_QUANT = 4
+W_LOADS = (1, 1, 1, 1, 1, 1, 1, 1)
+ROWS_AFTER = (2, 3, 8)
+V_WINDOWS = 1
+OFF = dict(y1=24, m0=136, m1=76, w0=12, w1=40, h0=124, h1=128)
+LOADS = [(0, 0), (0, 1), (1, 0), (2, 0), (1, 1), (2, 1)]
+W_CAST = ["s","s","s","v","s","s","s","sv"]
 
 
 def tile_attend_gkl_wx_ts_kb_kernel(tc, xT, wT, y, wt, ts, kb, xm, offs, out_0, out_1):
@@ -76,24 +81,30 @@ def tile_attend_gkl_wx_ts_kb_kernel(tc, xT, wT, y, wt, ts, kb, xm, offs, out_0, 
 
         ts_win, kb_win = at("ts_win", 32, T, F32), at("kb_win", 40, T, F32)
         wt_rows = keep.tile([P, P], F32, name="wt_rows")
-        nc.vector.memset(wt_rows[:], 0.0)
         nc.vector.memset(ts_win[:], 0.0)
         nc.vector.memset(kb_win[:], 0.0)
+        nc.vector.memset(wt_rows[:], 0.0)
         warm = keep.tile([P, 1], F32, name="warm")
-        nc.scalar.activation(warm[:], wt_rows[:, 0:1], ACT.Exp)
-        nc.scalar.dma_start(ts_win[0:1, :], ts[0:1, :])
-        nc.scalar.dma_start(kb_win[1:2, :], kb[1:2, :])
-        nc.scalar.dma_start(wt_rows[0:4 * B, :], wt.rearrange("b (j p) o -> (b j) (p o)", p=P))
         ident = keep.tile([P, P], F32, name="ident")
         make_identity(nc, ident[:])
+        nc.scalar.activation(warm[:], ident[:, 0:1], ACT.Exp)
 
         w_rows = wT.rearrange("(p u e) c -> p u e c", u=2, e=2)
-        w_raw = []
-        for u in range(2):
-            for c in range(0, T, CHUNK):
-                raw = at("w_raw%d" % len(w_raw), 4 * len(w_raw), 2 * CHUNK, F32)
-                nc.sync.dma_start(raw[:].rearrange("p (e c) -> p e c", e=2), w_rows[:, u, :, c:c + CHUNK])
-                w_raw.append(raw)
+        w_pieces = []
+        done = 0
+        for n, chunks in enumerate(W_LOADS):
+            u, c = divmod(done * CHUNK, T)
+            raw = at("w_raw%d" % n, 4 * done, 2 * chunks * CHUNK, F32)
+            rows = raw[:].rearrange("p (e c) -> p e c", e=2)
+            nc.sync.dma_start(rows, w_rows[:, u, :, c:c + chunks * CHUNK])
+            w_pieces.extend(rows[:, :, k * CHUNK:(k + 1) * CHUNK] for k in range(chunks))
+            done += chunks
+            if n + 1 == ROWS_AFTER[0]:
+                nc.sync.dma_start(ts_win[0:1, :], ts[0:1, :])
+            if n + 1 == ROWS_AFTER[1]:
+                nc.sync.dma_start(kb_win[1:2, :], kb[1:2, :])
+            if n + 1 == min(ROWS_AFTER[2], len(W_LOADS)):
+                nc.sync.dma_start(wt_rows[0:4 * B, :], wt.rearrange("b (j p) o -> (b j) (p o)", p=P))
         x_raw, y_raw, xm_raw = [], [], []
         for b in range(B):
             x_raw.append(at("x_raw%d" % b, 76 + 8 * b, 2048, F32))
@@ -101,7 +112,10 @@ def tile_attend_gkl_wx_ts_kb_kernel(tc, xT, wT, y, wt, ts, kb, xm, offs, out_0, 
             xm_raw.append(at("xm_raw%d" % b, 108 + 8 * b, 2048, F32))
 
         def load_x(b):
-            nc.sync.dma_start(x_raw[b][:], xT[b].rearrange("(p j) r -> p (j r)", j=4))
+            step = R // X_LOADS[b]
+            for c in range(0, R, step):
+                nc.sync.dma_start(x_raw[b][:].rearrange("p (j r) -> p j r", j=4)[:, :, c:c + step],
+                                  xT[b].rearrange("(p j) r -> p j r", j=4)[:, :, c:c + step])
 
         def load_y(b):
             nc.sync.dma_start(y_raw[b][:].rearrange("p (j i) -> p j i", j=4), y[b].rearrange("(j p) i -> p j i", p=P))
@@ -113,14 +127,14 @@ def tile_attend_gkl_wx_ts_kb_kernel(tc, xT, wT, y, wt, ts, kb, xm, offs, out_0, 
             (load_x, load_y, load_xm)[load](b)
 
         w_pairs = [at("w_pairs%d" % u, 60 + 8 * u, 2 * T, BF16) for u in range(2)]
-        for n, raw in enumerate(w_raw):
-            u, c = n // (T // CHUNK), (n % (T // CHUNK)) * CHUNK
+        for n, piece in enumerate(w_pieces):
+            u, c = divmod(n * CHUNK, T)
             engines = W_CAST[n]
             step = CHUNK // 4 // len(engines)
             for k, engine in enumerate(engines):
                 copy(engine,
                      w_pairs[u][:].rearrange("p (c i e) -> p c e i", e=2, i=4)[:, c // 4 + k * step:c // 4 + (k + 1) * step],
-                     raw[:].rearrange("p (e c i) -> p c e i", e=2, i=4)[:, k * step:(k + 1) * step])
+                     piece.rearrange("p e (c i) -> p c e i", i=4)[:, k * step:(k + 1) * step])
 
         wt_bank = bank("wt_bank", 7)
         nc.tensor.transpose(wt_bank[:, 0:P], wt_rows[:], ident[:])
@@ -131,9 +145,9 @@ def tile_attend_gkl_wx_ts_kb_kernel(tc, xT, wT, y, wt, ts, kb, xm, offs, out_0, 
         nc.vector.tensor_scalar_mul(neg_wt_cols[:], wt_bank[:, 0:4 * B], -1.0)
 
         windows = [keep.tile([P, T], F32, name="window%d" % k) for k in range(4)]
-        for window in windows:
+        for k, window in enumerate(windows):
             for c in range(0, T, 512):
-                nc.gpsimd.memset(window[:, c:c + 512], 0.0)
+                (nc.vector if k < V_WINDOWS else nc.gpsimd).memset(window[:, c:c + 512], 0.0)
 
         def gather(b, picked, u):
             nc.vector.tensor_copy(
@@ -158,7 +172,7 @@ def tile_attend_gkl_wx_ts_kb_kernel(tc, xT, wT, y, wt, ts, kb, xm, offs, out_0, 
         def quantize_w(b, picked, w_in, engine):
             copy(engine, w_in[:].rearrange("p (s u e) -> p s u e", u=2, e=2),
                  picked[:].bitcast(BF16).rearrange("p (u s e) -> p s u e", u=2, e=2))
-            return quantize("w%d" % b, w_in, E4M3, 2)
+            return quantize("w%d" % b, w_in, E4M3, (W_QUANT, 1)[b])
 
         def scores(b, half, w_q, x_q, cols, engines):
             a_t = at("a_t%d_%d" % (b, half), 8 * b + 4 * half, 1024, F32)
@@ -220,7 +234,7 @@ def tile_attend_gkl_wx_ts_kb_kernel(tc, xT, wT, y, wt, ts, kb, xm, offs, out_0, 
                 nc.scalar.activation(prob[:], prob[:], ACT.Copy, scale=factor[:, n:n + 1])
             return probs
 
-        def turn_and_scale(b, half, target, prob, cols, h_t):
+        def turn_and_scale(b, half, target, prob, cols, h_t, engines):
             h_tv = h_t[:].rearrange("p (t u m e) -> p t u m e", t=4, u=2, e=2)
             for tp in range(2):
                 turned = bank("turned%d_%d_%d" % (b, half, tp), 4 * b + 2 * half + tp)
@@ -233,12 +247,14 @@ def tile_attend_gkl_wx_ts_kb_kernel(tc, xT, wT, y, wt, ts, kb, xm, offs, out_0, 
                                 start=(term, jj, q) == (0, 0, 0), stop=(term, jj, q) == (1, 1, 1), is_transpose=True)
                 for q in range(2):
                     t = 2 * tp + q
-                    nc.scalar.activation(
-                        h_tv[:, t, :, half * 64:(half + 1) * 64, :],
-                        turned[:, q * 256:(q + 1) * 256].rearrange("p (m u e) -> p u m e", u=2, e=2),
-                        ACT.Copy, scale=cols[:, t, 0:1])
+                    dst = h_tv[:, t, :, half * 64:(half + 1) * 64, :]
+                    src = turned[:, q * 256:(q + 1) * 256].rearrange("p (m u e) -> p u m e", u=2, e=2)
+                    if engines[tp] == "s":
+                        nc.scalar.activation(dst, src, ACT.Copy, scale=cols[:, t, 0:1])
+                    else:
+                        nc.vector.tensor_scalar_mul(dst, src, cols[:, t, 0:1])
 
-        def quantize_h(b, h_t):
+        def quantize_h(b, h_t, engines):
             h_in = at("h_in%d" % b, 76 + 8 * b, 2048, BF16)
             h_words = h_t[:].bitcast(F32)
             h_inv = h_in[:].bitcast(F32).rearrange("p (g t a u) -> p t g a u", t=4, a=8, u=2)
@@ -247,7 +263,7 @@ def tile_attend_gkl_wx_ts_kb_kernel(tc, xT, wT, y, wt, ts, kb, xm, offs, out_0, 
                 for q in range(4):
                     nc.tensor.transpose(turned[:, q * P:(q + 1) * P], h_words[:, (4 * tp + q) * P:(4 * tp + q + 1) * P], ident[:])
                 for q in range(2):
-                    nc.scalar.copy(h_inv[:, 2 * tp + q], turned[:, q * 256:(q + 1) * 256].rearrange("p (u g a) -> p g a u", u=2, a=8))
+                    copy(engines[tp], h_inv[:, 2 * tp + q], turned[:, q * 256:(q + 1) * 256].rearrange("p (u g a) -> p g a u", u=2, a=8))
             return quantize("h%d" % b, h_in, E5M2, 1)
 
         def quantize_xm(b, engine):
@@ -257,9 +273,9 @@ def tile_attend_gkl_wx_ts_kb_kernel(tc, xT, wT, y, wt, ts, kb, xm, offs, out_0, 
             acc = bank("dw%d_%d" % (b, k), n)
             matmul(acc[:], xm_q, slice(k * P, (k + 1) * P), h_q, slice(0, N))
             staged = at("dw_staged%d_%d" % (b, k), 48 + 2 * ((4 * b + k) % 6), N, F32)
-            nc.scalar.copy(staged[:], acc[:])
             step = N // pieces
             for c in range(0, N, step):
+                nc.scalar.copy(staged[:, c:c + step], acc[:, c:c + step])
                 part = offsets[:, (b * N + c) // 16:(b * N + c + step) // 16]
                 nc.vector.tensor_copy(windows[k][:].indirect(part), staged[:, c:c + step])
             if b == B - 1:
@@ -292,68 +308,68 @@ def tile_attend_gkl_wx_ts_kb_kernel(tc, xT, wT, y, wt, ts, kb, xm, offs, out_0, 
 
         h_t = [at("h_t%d" % b, 144 + 4 * b, 2048, BF16) for b in range(B)]
         a_t, target, maxes, prob = [[{} for b in range(B)] for n in range(4)]
-        cols0 = token_columns(0)
-        x_q0 = quantize("x0", interleave(at("x_in0", 140, 2048, BF16), x_raw[0], "ss"), E4M3, 2)
-        cols1 = token_columns(1)
-        target[0][0] = targets(0, 0, "v")
         picked0 = at("picked0", 132, 2 * N, U32)
         gather(0, picked0, 0)
         gather(0, picked0, 1)
+        x_q0 = quantize("x0", interleave(at("x_in0", 140, 2048, BF16), x_raw[0], "ss"), E4M3, 2)
+        cols1 = token_columns(1)
         w_q0 = quantize_w(0, picked0, at("w_in0", 136, 2048, BF16), "v")
-        target[0][1] = targets(0, 1, "v")
-        a_t[0][1] = scores(0, 1, w_q0, x_q0, cols0, "ss")
-        a_t[0][0] = scores(0, 0, w_q0, x_q0, cols0, "ss")
-        maxes[0][0] = row_max(0, 0, a_t[0][0])
-        maxes[0][1] = row_max(0, 1, a_t[0][0])
-        x_q1 = quantize("x1", interleave(at("x_in1", 152, 2048, BF16), x_raw[1], "sv"), E4M3, 2)
-        target[0][3] = targets(0, 3, "s")
-        prob[0][0], prob[0][1] = weighted_on_scalar(0, (0, 1), maxes[0])
-        target[1][3] = targets(1, 3, "s")
+        target[0][0] = targets(0, 0, "v")
+        cols0 = token_columns(0)
+        target[0][2] = targets(0, 2, "s")
         picked1 = at("picked1", 140, 2 * N, U32)
         gather(1, picked1, 0)
         gather(1, picked1, 1)
-        w_q1 = quantize_w(1, picked1, at("w_in1", 156, 2048, BF16), "v")
+        target[0][1] = targets(0, 1, "v")
+        w_q1 = quantize_w(1, picked1, at("w_in1", 136, 2048, BF16), "v")
+        a_t[0][0] = scores(0, 0, w_q0, x_q0, cols0, "ss")
+        target[0][3] = targets(0, 3, "s")
+        a_t[0][1] = scores(0, 1, w_q0, x_q0, cols0, "ss")
+        x_q1 = quantize("x1", interleave(at("x_in1", 152, 2048, BF16), x_raw[1], "vs"), E4M3, 1)
+        maxes[0][1] = row_max(0, 1, a_t[0][0])
+        target[1][2] = targets(1, 2, "v")
         maxes[0][2] = row_max(0, 2, a_t[0][1])
-        maxes[0][3] = row_max(0, 3, a_t[0][1])
-        a_t[1][0] = scores(1, 0, w_q1, x_q1, cols1, "vv")
-        prob[0][2] = weighted_on_vector(0, 2, maxes[0])
-        prob[0][3] = weighted_on_vector(0, 3, maxes[0])
-        maxes[1][0] = row_max(1, 0, a_t[1][0])
-        target[1][0] = targets(1, 0, "v")
-        xm_q0 = quantize_xm(0, "vv")
         a_t[1][1] = scores(1, 1, w_q1, x_q1, cols1, "vv")
-        target[0][2] = targets(0, 2, "s")
+        maxes[0][3] = row_max(0, 3, a_t[0][1])
+        prob[0][2], prob[0][3] = weighted_on_scalar(0, (2, 3), maxes[0])
+        maxes[0][0] = row_max(0, 0, a_t[0][0])
+        xm_q0 = quantize_xm(0, "vs")
+        prob[0][0] = weighted_on_vector(0, 0, maxes[0])
+        prob[0][1] = weighted_on_vector(0, 1, maxes[0])
+        a_t[1][0] = scores(1, 0, w_q1, x_q1, cols1, "vv")
         maxes[1][3] = row_max(1, 3, a_t[1][1])
-        turn_and_scale(0, 0, target[0], prob[0], cols0, h_t[0])
         maxes[1][2] = row_max(1, 2, a_t[1][1])
-        target[1][2] = targets(1, 2, "s")
-        turn_and_scale(0, 1, target[0], prob[0], cols0, h_t[0])
+        turn_and_scale(0, 1, target[0], prob[0], cols0, h_t[0], "ss")
+        xm_q1 = quantize_xm(1, "vv")
+        maxes[1][0] = row_max(1, 0, a_t[1][0])
+        turn_and_scale(0, 0, target[0], prob[0], cols0, h_t[0], "ss")
+        h_q0 = quantize_h(0, h_t[0], "vs")
         maxes[1][1] = row_max(1, 1, a_t[1][0])
-        h_q0 = quantize_h(0, h_t[0])
-        table_gradient(0, 1, 0, xm_q0, h_q0, 1)
-        prob[1][2], prob[1][3] = weighted_on_scalar(1, (2, 3), maxes[1])
-        h_tq0 = quantize_h_turned(0, h_t[0], "vs")
+        target[1][1] = targets(1, 1, "s")
+        h_tq0 = quantize_h_turned(0, h_t[0], "vv")
+        target[1][0] = targets(1, 0, "s")
+        table_gradient(0, 0, 3, xm_q0, h_q0, 1)
         prob[1][0], prob[1][1] = weighted_on_scalar(1, (0, 1), maxes[1])
-        target[1][1] = targets(1, 1, "v")
-        table_gradient(0, 0, 4, xm_q0, h_q0, 1)
-        xm_q1 = quantize_xm(1, "sv")
-        turn_and_scale(1, 1, target[1], prob[1], cols1, h_t[1])
-        table_gradient(0, 2, 3, xm_q0, h_q0, 1)
-        turn_and_scale(1, 0, target[1], prob[1], cols1, h_t[1])
-        h_q1 = quantize_h(1, h_t[1])
-        table_gradient(0, 3, 4, xm_q0, h_q0, 1)
+        prob[1][2], prob[1][3] = weighted_on_scalar(1, (2, 3), maxes[1])
+        table_gradient(0, 1, 3, xm_q0, h_q0, 1)
+        target[1][3] = targets(1, 3, "v")
+        turn_and_scale(1, 0, target[1], prob[1], cols1, h_t[1], "ss")
+        w_tq0 = quantize_w_turned(0, picked0, (7, 1))
+        table_gradient(0, 2, 0, xm_q0, h_q0, 1)
+        turn_and_scale(1, 1, target[1], prob[1], cols1, h_t[1], "ss")
+        row_gradient(0, 2, 5, h_tq0, w_tq0)
+        h_q1 = quantize_h(1, h_t[1], "ss")
         w_tq1 = quantize_w_turned(1, picked1, (5, 0))
+        table_gradient(0, 3, 6, xm_q0, h_q0, 1)
         h_tq1 = quantize_h_turned(1, h_t[1], "ss")
-        row_gradient(1, 0, 0, h_tq1, w_tq1)
-        table_gradient(1, 0, 3, xm_q1, h_q1, 1)
-        w_tq0 = quantize_w_turned(0, picked0, (4, 7))
-        table_gradient(1, 3, 2, xm_q1, h_q1, 1)
-        table_gradient(1, 1, 5, xm_q1, h_q1, 1)
-        row_gradient(1, 3, 1, h_tq1, w_tq1)
-        row_gradient(1, 2, 3, h_tq1, w_tq1)
-        row_gradient(0, 1, 1, h_tq0, w_tq0)
+        row_gradient(0, 0, 4, h_tq0, w_tq0)
+        row_gradient(0, 1, 4, h_tq0, w_tq0)
+        table_gradient(1, 0, 7, xm_q1, h_q1, 1)
+        row_gradient(1, 0, 4, h_tq1, w_tq1)
+        table_gradient(1, 3, 6, xm_q1, h_q1, 1)
+        table_gradient(1, 2, 5, xm_q1, h_q1, 1)
+        row_gradient(1, 3, 7, h_tq1, w_tq1)
         row_gradient(1, 1, 4, h_tq1, w_tq1)
-        row_gradient(0, 0, 1, h_tq0, w_tq0)
-        row_gradient(0, 3, 3, h_tq0, w_tq0)
-        row_gradient(0, 2, 4, h_tq0, w_tq0)
-        table_gradient(1, 2, 7, xm_q1, h_q1, 1)
+        row_gradient(0, 3, 1, h_tq0, w_tq0)
+        row_gradient(1, 2, 5, h_tq1, w_tq1)
+        table_gradient(1, 1, 1, xm_q1, h_q1, 1)

from contextlib import ExitStack

import concourse.mybir as mybir
from concourse.masks import make_identity

B, N, T, D, R = 2, 512, 2048, 512, 512
P = 128
FLOPS = 3 * 2 * B * D * R * N
BYTES = 4 * (3 * B * D * R + D * T + B * R + 2 * T + D * T + B * R * D) + 2 * P * B * N // 16

F32 = mybir.dt.float32
BF16 = mybir.dt.bfloat16
U32 = mybir.dt.uint32
U16 = mybir.dt.uint16
U8 = mybir.dt.uint8
E4M3 = mybir.dt.float8_e4m3fn_x4
E5M2 = mybir.dt.float8_e5m2_x4
ALU = mybir.AluOpType
ACT = mybir.ActivationFunctionType
AXIS = mybir.AxisListType

CHUNK = 512
X_LOADS = (2, 1)
W_QUANT = 4
W_LOADS = (1, 1, 1, 1, 1, 1, 1, 1)
ROWS_AFTER = (2, 3, 8)
V_WINDOWS = 1
OFF = dict(y1=24, m0=136, m1=76, w0=12, w1=40, h0=124, h1=128)
LOADS = [(0, 0), (0, 1), (1, 0), (2, 0), (1, 1), (2, 1)]
W_CAST = ["s","s","s","v","s","s","s","sv"]


def tile_attend_gkl_wx_ts_kb_kernel(tc, xT, wT, y, wt, ts, kb, xm, offs, out_0, out_1):
    nc = tc.nc
    with ExitStack() as ctx:
        keep = ctx.enter_context(tc.tile_pool(name="keep", bufs=1))
        arena = ctx.enter_context(tc.tile_pool(name="arena", bufs=1))
        psum = ctx.enter_context(tc.psum_pool(name="psum", bufs=1))

        def at(name, kib, cols, dtype):
            return arena.tile([P, cols], dtype, name=name, offset=int(kib * 1024), align_bytes=64)

        def bank(name, n):
            return psum.tile([P, 512], F32, name=name, offset=n * 2048)

        def copy(engine, out, in_):
            if engine == "s":
                nc.scalar.copy(out, in_)
            else:
                nc.vector.tensor_copy(out, in_)

        def quantize(name, src, fmt, pieces):
            codes = keep.tile([P, 512], U32, name=name + "_codes", align_bytes=64)
            scales = keep.tile([P, 512], U8, name=name + "_scales", align_bytes=64)
            step = 512 // pieces
            for c in range(0, 512, step):
                nc.vector.quantize_mx(codes[:, c:c + step].bitcast(fmt), scales[:, c:c + step], src[:, 4 * c:4 * (c + step)])
            return codes, scales, fmt

        def matmul(out, lhs, lhs_cols, rhs, rhs_cols):
            nc.tensor.matmul_mx(
                out,
                lhsT=lhs[0][:, lhs_cols].bitcast(lhs[2]), lhsT_scale=lhs[1][:, lhs_cols],
                rhs=rhs[0][:, rhs_cols].bitcast(rhs[2]), rhs_scale=rhs[1][:, rhs_cols],
                start=True, stop=True,
            )

        def interleave(dst, raw, engines):
            src_v = raw[:].rearrange("p (j c i) -> p c j i", j=4, i=4)
            dst_v = dst[:].rearrange("p (c i j) -> p c j i", j=4, i=4)
            step = 128 // len(engines)
            for k, engine in enumerate(engines):
                copy(engine, dst_v[:, k * step:(k + 1) * step], src_v[:, k * step:(k + 1) * step])
            return dst

        offsets = keep.tile([P, B * N // 16], U16, name="offsets")
        nc.sync.dma_start(offsets[:], offs)

        def listed(window, b):
            return window.indirect(offsets[:, b * (N // 16):(b + 1) * (N // 16)])

        ts_win, kb_win = at("ts_win", 32, T, F32), at("kb_win", 40, T, F32)
        wt_rows = keep.tile([P, P], F32, name="wt_rows")
        nc.vector.memset(ts_win[:], 0.0)
        nc.vector.memset(kb_win[:], 0.0)
        nc.vector.memset(wt_rows[:], 0.0)
        warm = keep.tile([P, 1], F32, name="warm")
        ident = keep.tile([P, P], F32, name="ident")
        make_identity(nc, ident[:])
        nc.scalar.activation(warm[:], ident[:, 0:1], ACT.Exp)

        w_rows = wT.rearrange("(p u e) c -> p u e c", u=2, e=2)
        w_pieces = []
        done = 0
        for n, chunks in enumerate(W_LOADS):
            u, c = divmod(done * CHUNK, T)
            raw = at("w_raw%d" % n, 4 * done, 2 * chunks * CHUNK, F32)
            rows = raw[:].rearrange("p (e c) -> p e c", e=2)
            nc.sync.dma_start(rows, w_rows[:, u, :, c:c + chunks * CHUNK])
            w_pieces.extend(rows[:, :, k * CHUNK:(k + 1) * CHUNK] for k in range(chunks))
            done += chunks
            if n + 1 == ROWS_AFTER[0]:
                nc.sync.dma_start(ts_win[0:1, :], ts[0:1, :])
            if n + 1 == ROWS_AFTER[1]:
                nc.sync.dma_start(kb_win[1:2, :], kb[1:2, :])
            if n + 1 == min(ROWS_AFTER[2], len(W_LOADS)):
                nc.sync.dma_start(wt_rows[0:4 * B, :], wt.rearrange("b (j p) o -> (b j) (p o)", p=P))
        x_raw, y_raw, xm_raw = [], [], []
        for b in range(B):
            x_raw.append(at("x_raw%d" % b, 76 + 8 * b, 2048, F32))
            y_raw.append(at("y_raw%d" % b, 92 + 8 * b, 2048, F32))
            xm_raw.append(at("xm_raw%d" % b, 108 + 8 * b, 2048, F32))

        def load_x(b):
            step = R // X_LOADS[b]
            for c in range(0, R, step):
                nc.sync.dma_start(x_raw[b][:].rearrange("p (j r) -> p j r", j=4)[:, :, c:c + step],
                                  xT[b].rearrange("(p j) r -> p j r", j=4)[:, :, c:c + step])

        def load_y(b):
            nc.sync.dma_start(y_raw[b][:].rearrange("p (j i) -> p j i", j=4), y[b].rearrange("(j p) i -> p j i", p=P))

        def load_xm(b):
            nc.sync.dma_start(xm_raw[b][:], xm[b].rearrange("(p j) d -> p (j d)", j=4))

        for load, b in LOADS:
            (load_x, load_y, load_xm)[load](b)

        w_pairs = [at("w_pairs%d" % u, 60 + 8 * u, 2 * T, BF16) for u in range(2)]
        for n, piece in enumerate(w_pieces):
            u, c = divmod(n * CHUNK, T)
            engines = W_CAST[n]
            step = CHUNK // 4 // len(engines)
            for k, engine in enumerate(engines):
                copy(engine,
                     w_pairs[u][:].rearrange("p (c i e) -> p c e i", e=2, i=4)[:, c // 4 + k * step:c // 4 + (k + 1) * step],
                     piece.rearrange("p e (c i) -> p c e i", i=4)[:, k * step:(k + 1) * step])

        wt_bank = bank("wt_bank", 7)
        nc.tensor.transpose(wt_bank[:, 0:P], wt_rows[:], ident[:])
        wt_cols = keep.tile([P, 4 * B], F32, name="wt_cols")
        nc.vector.tensor_copy(wt_cols[:], wt_bank[:, 0:4 * B])

        neg_wt_cols = keep.tile([P, 4 * B], F32, name="neg_wt_cols")
        nc.vector.tensor_scalar_mul(neg_wt_cols[:], wt_bank[:, 0:4 * B], -1.0)

        windows = [keep.tile([P, T], F32, name="window%d" % k) for k in range(4)]
        for k, window in enumerate(windows):
            for c in range(0, T, 512):
                (nc.vector if k < V_WINDOWS else nc.gpsimd).memset(window[:, c:c + 512], 0.0)

        def gather(b, picked, u):
            nc.vector.tensor_copy(
                picked[:, u * N:(u + 1) * N].rearrange("p (t g a) -> p g t a", t=4, a=8),
                listed(w_pairs[u][:].bitcast(U32), b))

        def token_columns(b):
            ts_g, kb_g, both = [at("tok%d_%d" % (b, i), 48 + 6 * b + 2 * i, N, F32) for i in range(3)]
            nc.vector.tensor_copy(ts_g[:], listed(ts_win[:], b))
            nc.vector.tensor_copy(kb_g[:], listed(kb_win[:], b))
            nc.vector.tensor_tensor(
                both[:].rearrange("p (t g a) -> p t g a", t=4, a=8),
                ts_g[:].rearrange("p (g t a) -> p t g a", t=4, a=8),
                kb_g[:].rearrange("p (g t a) -> p t g a", t=4, a=8), ALU.add)
            turned = bank("tok_bank%d" % b, 5 + b)
            for t in range(4):
                nc.tensor.transpose(turned[:, t * P:(t + 1) * P], both[:, t * P:(t + 1) * P], ident[:])
            cols = keep.tile([P, 4, 2], F32, name="tok_cols%d" % b)
            nc.vector.tensor_copy(cols[:], turned[:].rearrange("p (t q) -> p t q", t=4)[:, :, 0:2])
            return cols

        def quantize_w(b, picked, w_in, engine):
            copy(engine, w_in[:].rearrange("p (s u e) -> p s u e", u=2, e=2),
                 picked[:].bitcast(BF16).rearrange("p (u s e) -> p s u e", u=2, e=2))
            return quantize("w%d" % b, w_in, E4M3, (W_QUANT, 1)[b])

        def scores(b, half, w_q, x_q, cols, engines):
            a_t = at("a_t%d_%d" % (b, half), 8 * b + 4 * half, 1024, F32)
            for tp in range(2):
                acc = bank("scores%d_%d_%d" % (b, half, tp), 4 * b + 2 * half + tp)
                for q in range(2):
                    t = 2 * tp + q
                    matmul(acc[:, q * 256:(q + 1) * 256], w_q, slice(t * P, (t + 1) * P), x_q, slice(half * 256, (half + 1) * 256))
                for q in range(2):
                    t = 2 * tp + q
                    dst, src = a_t[:, t * 256:(t + 1) * 256], acc[:, q * 256:(q + 1) * 256]
                    if engines[tp] == "s":
                        nc.scalar.activation(dst, src, ACT.Identity, bias=cols[:, t, 1:2], scale=cols[:, t, 0:1])
                    else:
                        nc.vector.tensor_scalar(dst, src, cols[:, t, 0:1], cols[:, t, 1:2], ALU.mult, ALU.add)
            return a_t

        def targets(b, j, engine):
            target = at("target%d_%d" % (b, j), (16, OFF["y1"])[b] + 2 * j, N, F32)
            dst = target[:].rearrange("p (t g a) -> p t g a", t=4, a=8)
            src = y_raw[b][:, j * N:(j + 1) * N].rearrange("p (g t a) -> p t g a", t=4, a=8)
            if engine == "s":
                nc.scalar.activation(dst, src, ACT.Copy, scale=neg_wt_cols[:, 4 * b + j:4 * b + j + 1])
            else:
                nc.vector.tensor_scalar_mul(dst, src, neg_wt_cols[:, 4 * b + j:4 * b + j + 1])
            return target

        def row_max(b, j, a_t):
            rows = bank("rows%d_%d" % (b, j), 4 * b + j)
            jj = j % 2
            for t in range(4):
                nc.tensor.transpose(rows[:, t * P:(t + 1) * P], a_t[:, t * 256 + jj * P:t * 256 + (jj + 1) * P], ident[:])
            neg_max = keep.tile([P, 1], F32, name="neg_max%d_%d" % (b, j))
            nc.vector.tensor_reduce(neg_max[:], rows[:], AXIS.X, ALU.max, negate=True)
            return rows, neg_max

        def exponentials(b, j, rows, neg_max, total):
            prob = at("prob%d_%d" % (b, j), 32 + 8 * b + 2 * j, N, F32)
            nc.scalar.activation(prob[:], rows[:], ACT.Exp, bias=neg_max[:], scale=1.0, accum_out=total)
            return prob

        def weighted_on_vector(b, j, maxes):
            rows, neg_max = maxes[j]
            total = keep.tile([P, 1], F32, name="total%d_%d" % (b, j))
            inverse = keep.tile([P, 1], F32, name="inverse%d_%d" % (b, j))
            prob = exponentials(b, j, rows, neg_max, total[:])
            nc.vector.reciprocal(inverse[:], total[:])
            nc.vector.tensor_scalar(prob[:], prob[:], inverse[:], wt_cols[:, 4 * b + j:4 * b + j + 1], ALU.mult, ALU.mult)
            return prob

        def weighted_on_scalar(b, js, maxes):
            total = keep.tile([P, len(js)], F32, name="totals%d_%d" % (b, js[0]))
            inverse = keep.tile([P, len(js)], F32, name="inverses%d_%d" % (b, js[0]))
            factor = keep.tile([P, len(js)], F32, name="factors%d_%d" % (b, js[0]))
            probs = [exponentials(b, j, *maxes[j], total[:, n:n + 1]) for n, j in enumerate(js)]
            nc.vector.reciprocal(inverse[:], total[:])
            nc.vector.tensor_tensor(factor[:], inverse[:], wt_cols[:, 4 * b + js[0]:4 * b + js[-1] + 1], ALU.mult)
            for n, prob in enumerate(probs):
                nc.scalar.activation(prob[:], prob[:], ACT.Copy, scale=factor[:, n:n + 1])
            return probs

        def turn_and_scale(b, half, target, prob, cols, h_t, engines):
            h_tv = h_t[:].rearrange("p (t u m e) -> p t u m e", t=4, u=2, e=2)
            for tp in range(2):
                turned = bank("turned%d_%d_%d" % (b, half, tp), 4 * b + 2 * half + tp)
                for term, tiles in enumerate((target, prob)):
                    for jj in range(2):
                        for q in range(2):
                            t = 2 * tp + q
                            nc.tensor.matmul(
                                turned[:, q * 256 + jj * P:q * 256 + (jj + 1) * P], tiles[2 * half + jj][:, t * P:(t + 1) * P], ident[:],
                                start=(term, jj, q) == (0, 0, 0), stop=(term, jj, q) == (1, 1, 1), is_transpose=True)
                for q in range(2):
                    t = 2 * tp + q
                    dst = h_tv[:, t, :, half * 64:(half + 1) * 64, :]
                    src = turned[:, q * 256:(q + 1) * 256].rearrange("p (m u e) -> p u m e", u=2, e=2)
                    if engines[tp] == "s":
                        nc.scalar.activation(dst, src, ACT.Copy, scale=cols[:, t, 0:1])
                    else:
                        nc.vector.tensor_scalar_mul(dst, src, cols[:, t, 0:1])

        def quantize_h(b, h_t, engines):
            h_in = at("h_in%d" % b, 76 + 8 * b, 2048, BF16)
            h_words = h_t[:].bitcast(F32)
            h_inv = h_in[:].bitcast(F32).rearrange("p (g t a u) -> p t g a u", t=4, a=8, u=2)
            for tp in range(2):
                turned = bank("h_words%d_%d" % (b, tp), 4 * b + tp)
                for q in range(4):
                    nc.tensor.transpose(turned[:, q * P:(q + 1) * P], h_words[:, (4 * tp + q) * P:(4 * tp + q + 1) * P], ident[:])
                for q in range(2):
                    copy(engines[tp], h_inv[:, 2 * tp + q], turned[:, q * 256:(q + 1) * 256].rearrange("p (u g a) -> p g a u", u=2, a=8))
            return quantize("h%d" % b, h_in, E5M2, 1)

        def quantize_xm(b, engine):
            return quantize("xm%d" % b, interleave(at("xm_in%d" % b, OFF["m%d" % b], 2048, BF16), xm_raw[b], engine), E4M3, 1)

        def table_gradient(b, k, n, xm_q, h_q, pieces):
            acc = bank("dw%d_%d" % (b, k), n)
            matmul(acc[:], xm_q, slice(k * P, (k + 1) * P), h_q, slice(0, N))
            staged = at("dw_staged%d_%d" % (b, k), 48 + 2 * ((4 * b + k) % 6), N, F32)
            step = N // pieces
            for c in range(0, N, step):
                nc.scalar.copy(staged[:, c:c + step], acc[:, c:c + step])
                part = offsets[:, (b * N + c) // 16:(b * N + c + step) // 16]
                nc.vector.tensor_copy(windows[k][:].indirect(part), staged[:, c:c + step])
            if b == B - 1:
                nc.sync.dma_start(out_0[k * P:(k + 1) * P, :], windows[k][:])

        def quantize_w_turned(b, picked, banks):
            w_t = at("w_t%d" % b, OFF["w%d" % b], 2048, BF16)
            w_tv = w_t[:].rearrange("p (m u e t) -> p u m e t", u=2, e=2, t=4)
            words = picked[:].bitcast(F32)
            for u in range(2):
                turned = bank("w_words%d_%d" % (b, u), banks[u])
                for t in range(4):
                    nc.tensor.transpose(turned[:, t * P:(t + 1) * P], words[:, (4 * u + t) * P:(4 * u + t + 1) * P], ident[:])
                nc.scalar.copy(w_tv[:, u], turned[:].bitcast(BF16).rearrange("p (t m e) -> p m e t", t=4, e=2))
            return quantize("w_t%d" % b, w_t, E4M3, 1)

        def quantize_h_turned(b, h_t, engines):
            h_ti = at("h_ti%d" % b, OFF["h%d" % b], 2048, BF16)
            for u in range(2):
                copy(engines[u], h_ti[:].rearrange("p (m u e t) -> p u m e t", u=2, e=2, t=4)[:, u],
                     h_t[:].rearrange("p (t u m e) -> p u m e t", t=4, u=2, e=2)[:, u])
            return quantize("h_t%d" % b, h_ti, E5M2, 1)

        def row_gradient(b, j, n, h_tq, w_tq):
            acc = bank("gx%d_%d" % (b, j), n)
            matmul(acc[:], h_tq, slice(j * P, (j + 1) * P), w_tq, slice(0, D))
            staged = at("gx_staged%d_%d" % (b, j), 60 + 8 * b + 2 * j, D, F32)
            nc.scalar.copy(staged[:], acc[:])
            nc.scalar.dma_start(out_1[b, j * P:(j + 1) * P, :], staged[:])

        h_t = [at("h_t%d" % b, 144 + 4 * b, 2048, BF16) for b in range(B)]
        a_t, target, maxes, prob = [[{} for b in range(B)] for n in range(4)]
        picked0 = at("picked0", 132, 2 * N, U32)
        gather(0, picked0, 0)
        gather(0, picked0, 1)
        x_q0 = quantize("x0", interleave(at("x_in0", 140, 2048, BF16), x_raw[0], "ss"), E4M3, 2)
        cols1 = token_columns(1)
        w_q0 = quantize_w(0, picked0, at("w_in0", 136, 2048, BF16), "v")
        target[0][0] = targets(0, 0, "v")
        cols0 = token_columns(0)
        target[0][2] = targets(0, 2, "s")
        picked1 = at("picked1", 140, 2 * N, U32)
        gather(1, picked1, 0)
        gather(1, picked1, 1)
        target[0][1] = targets(0, 1, "v")
        w_q1 = quantize_w(1, picked1, at("w_in1", 136, 2048, BF16), "v")
        a_t[0][0] = scores(0, 0, w_q0, x_q0, cols0, "ss")
        target[0][3] = targets(0, 3, "s")
        a_t[0][1] = scores(0, 1, w_q0, x_q0, cols0, "ss")
        x_q1 = quantize("x1", interleave(at("x_in1", 152, 2048, BF16), x_raw[1], "vs"), E4M3, 1)
        maxes[0][1] = row_max(0, 1, a_t[0][0])
        target[1][2] = targets(1, 2, "v")
        maxes[0][2] = row_max(0, 2, a_t[0][1])
        a_t[1][1] = scores(1, 1, w_q1, x_q1, cols1, "vv")
        maxes[0][3] = row_max(0, 3, a_t[0][1])
        prob[0][2], prob[0][3] = weighted_on_scalar(0, (2, 3), maxes[0])
        maxes[0][0] = row_max(0, 0, a_t[0][0])
        xm_q0 = quantize_xm(0, "vs")
        prob[0][0] = weighted_on_vector(0, 0, maxes[0])
        prob[0][1] = weighted_on_vector(0, 1, maxes[0])
        a_t[1][0] = scores(1, 0, w_q1, x_q1, cols1, "vv")
        maxes[1][3] = row_max(1, 3, a_t[1][1])
        maxes[1][2] = row_max(1, 2, a_t[1][1])
        turn_and_scale(0, 1, target[0], prob[0], cols0, h_t[0], "ss")
        xm_q1 = quantize_xm(1, "vv")
        maxes[1][0] = row_max(1, 0, a_t[1][0])
        turn_and_scale(0, 0, target[0], prob[0], cols0, h_t[0], "ss")
        h_q0 = quantize_h(0, h_t[0], "vs")
        maxes[1][1] = row_max(1, 1, a_t[1][0])
        target[1][1] = targets(1, 1, "s")
        h_tq0 = quantize_h_turned(0, h_t[0], "vv")
        target[1][0] = targets(1, 0, "s")
        table_gradient(0, 0, 3, xm_q0, h_q0, 1)
        prob[1][0], prob[1][1] = weighted_on_scalar(1, (0, 1), maxes[1])
        prob[1][2], prob[1][3] = weighted_on_scalar(1, (2, 3), maxes[1])
        table_gradient(0, 1, 3, xm_q0, h_q0, 1)
        target[1][3] = targets(1, 3, "v")
        turn_and_scale(1, 0, target[1], prob[1], cols1, h_t[1], "ss")
        w_tq0 = quantize_w_turned(0, picked0, (7, 1))
        table_gradient(0, 2, 0, xm_q0, h_q0, 1)
        turn_and_scale(1, 1, target[1], prob[1], cols1, h_t[1], "ss")
        row_gradient(0, 2, 5, h_tq0, w_tq0)
        h_q1 = quantize_h(1, h_t[1], "ss")
        w_tq1 = quantize_w_turned(1, picked1, (5, 0))
        table_gradient(0, 3, 6, xm_q0, h_q0, 1)
        h_tq1 = quantize_h_turned(1, h_t[1], "ss")
        row_gradient(0, 0, 4, h_tq0, w_tq0)
        row_gradient(0, 1, 4, h_tq0, w_tq0)
        table_gradient(1, 0, 7, xm_q1, h_q1, 1)
        row_gradient(1, 0, 4, h_tq1, w_tq1)
        table_gradient(1, 3, 6, xm_q1, h_q1, 1)
        table_gradient(1, 2, 5, xm_q1, h_q1, 1)
        row_gradient(1, 3, 7, h_tq1, w_tq1)
        row_gradient(1, 1, 4, h_tq1, w_tq1)
        row_gradient(0, 3, 1, h_tq0, w_tq0)
        row_gradient(1, 2, 5, h_tq1, w_tq1)
        table_gradient(1, 1, 1, xm_q1, h_q1, 1)
